import numpy as np
import ml_dtypes


def mxq(x, axis, fmt="e4m3"):
    dtype, down = {"e4m3": (ml_dtypes.float8_e4m3fn, 7), "e5m2": (ml_dtypes.float8_e5m2, 14)}[fmt]
    v = np.moveaxis(np.asarray(x, np.float32).astype(ml_dtypes.bfloat16).astype(np.float64), axis, -1)
    blocks = v.reshape(v.shape[:-1] + (-1, 32))
    amax = np.abs(blocks).max(-1, keepdims=True)
    byte = np.maximum(np.where(amax > 0, np.frexp(amax)[1] - 1 + 127, 0) - down, 1)
    scale = np.exp2(byte - 127.0)
    codes = (blocks / scale).astype(np.float32).astype(dtype).astype(np.float64)
    return np.moveaxis((codes * scale).reshape(v.shape), -1, axis)


WIDE = False


def mx_kscale(k):
    if not WIDE:
        return np.ones(k)
    levels = np.array([10, -10, 5, -5, 0])
    if k % 512:
        return np.exp2(np.random.permutation(np.resize(levels, k // 32))).repeat(32)
    a = np.empty((k // 512, 16))
    for p in range(k // 512):
        a[p, :8] = np.random.permutation(np.resize(levels, 8))
        for g in range(8):
            far = levels[np.abs(levels - a[p, g]) >= 10]
            a[p, g + 8] = far[np.random.randint(len(far))]
    return np.exp2(a.ravel()).repeat(32)


def f64(x):
    return np.asarray(x).astype(np.float64)


def striped(idx):
    return np.tile(idx.reshape(-1, 16).T, (8, 1)).astype(np.uint16)


def unstriped(offs):
    return offs[:16].T.reshape(-1).astype(np.int64)


def striped8(idx):
    return np.concatenate([x.reshape(-1, 16).T for x in idx]).astype(np.uint16)


def runs(offs, k):
    lists = np.stack([offs[16 * r : 16 * r + 16].T.reshape(-1) for r in range(8)]).astype(np.int64)
    return lists[np.arange(k) % 512 // 64]


def pack_weight(w):
    k, n = w.shape
    w = f64(np.asarray(w, np.float32).astype(ml_dtypes.bfloat16)).reshape(k // 32, 32, n)
    amax = np.abs(w).max(1)
    byte = np.clip(np.where(amax > 0, np.frexp(amax)[1] - 1 + 127 - 7, 1), 1, 254)
    scaled = (w * np.exp2(127.0 - byte)[:, None, :]).reshape(k, n).astype(np.float32)
    words = np.ascontiguousarray(scaled.reshape(k // 512, 128, 4, n).transpose(0, 1, 3, 2)).astype(ml_dtypes.float8_e4m3fn).view(np.uint8)
    return words, np.ascontiguousarray(byte.astype(np.uint8).reshape(k // 512, 16, n))


def unpack_weight(words, scales):
    g, p, n, _ = words.shape
    vals = np.ascontiguousarray(words).view(ml_dtypes.float8_e4m3fn).astype(np.float64) * np.repeat(np.exp2(scales.astype(np.float64) - 127.0), 8, axis=1)[..., None]
    return vals.transpose(0, 1, 3, 2).reshape(g * 512, n)


E2M1 = np.array([0.0, 0.5, 1.0, 1.5, 2.0, 3.0, 4.0, 6.0, -0.0, -0.5, -1.0, -1.5, -2.0, -3.0, -4.0, -6.0])


def pack_fp4(w):
    k, n = w.shape
    w = f64(np.asarray(w, np.float32).astype(ml_dtypes.bfloat16)).reshape(k // 32, 32, n)
    amax = np.abs(w).max(1)
    mant, ex = np.frexp(amax / 6.0)
    byte = np.clip(np.where(amax > 0, np.where(mant > 0.5, ex, ex - 1) + 127, 1), 1, 254)
    scaled = (w * np.exp2(127.0 - byte)[:, None, :]).reshape(k, n).astype(np.float32)
    c = np.ascontiguousarray(scaled.reshape(k // 512, 128, 4, n).transpose(0, 1, 3, 2)).astype(ml_dtypes.float4_e2m1fn).view(np.uint8) & 0xF
    words = (c[..., 0::2] | (c[..., 1::2] << 4)).reshape(k // 512, 128, 2 * n)
    return np.ascontiguousarray(words), np.ascontiguousarray(byte.astype(np.uint8).reshape(k // 512, 16, n))


def unpack_fp4(words, scales):
    g, _, n = scales.shape
    words = np.ascontiguousarray(words).reshape(g, 128, n, 2)
    nib = np.empty((g, 128, n, 4), np.uint8)
    nib[..., 0::2] = words & 0xF
    nib[..., 1::2] = words >> 4
    vals = E2M1[nib] * np.repeat(np.exp2(scales.astype(np.float64) - 127.0), 8, axis=1)[..., None]
    return vals.transpose(0, 1, 3, 2).reshape(g * 512, n)


def planes(y):
    n, m = y.shape
    v = y.astype(np.float32).astype(ml_dtypes.bfloat16).astype(np.float64).reshape(n // 32, 32, m)
    top = np.abs(v).max(1)
    byte = np.clip(np.where(top > 0, np.frexp(top)[1] - 1 + 127 - 7, 1), 1, 254)
    codes = (v * np.exp2(127.0 - byte)[:, None, :]).reshape(n, m).astype(np.float32).astype(ml_dtypes.float8_e4m3fn).view(np.uint8)
    words = codes.reshape(n // 512, 128, 4, m).transpose(0, 1, 3, 2)
    return np.ascontiguousarray(words), np.ascontiguousarray(byte.astype(np.uint8).reshape(n // 512, 16, m))


K, T, S, N, H = 512, 2048, 512, 512, 512


def setup_inputs():
    n = np.random.standard_normal
    s = mx_kscale(K)[:, None]
    u = mx_kscale(H)
    packed_xT = pack_weight(n((K, T)) * s)
    packed_w1 = pack_fp4(n((K, H)) / np.sqrt(K) / s)
    packed_w2 = pack_fp4(n((H, N)) / np.sqrt(H) / u[:, None])
    return {
        "x_words": packed_xT[0],
        "x_scales": packed_xT[1],
        "w1_words": packed_w1[0],
        "w1_scales": packed_w1[1],
        "gn": (np.random.uniform(0.5, 1.5, (H, 1)) * u[:, None]).astype(np.float32),
        "w2_words": packed_w2[0],
        "w2_scales": packed_w2[1],
        "offs": striped(np.random.permutation(T)[:S]),
        "n1": striped8(np.stack([np.random.permutation(S) for _ in range(8)])),
        "n2": striped8(np.stack([np.random.permutation(S) for _ in range(8)])),
        "n3": striped8(np.stack([np.random.permutation(S) for _ in range(8)])),
        "n4": striped8(np.stack([np.random.permutation(S) for _ in range(8)])),
    }


def reference(x_words, x_scales, w1_words, w1_scales, gn, w2_words, w2_scales, offs, n1, n2, n3, n4):
    xq = unpack_weight(x_words, x_scales)[:, unstriped(offs)]
    y = unpack_fp4(w1_words, w1_scales).T @ xq
    ex = np.exp(0.5 * y)
    z = f64(gn) * ((ex * (y[np.arange(H)[:, None], runs(n1, H)])) / (ex + ex[np.arange(H)[:, None], runs(n2, H)]))
    h = unpack_fp4(w2_words, w2_scales).T @ mxq(z, 0, "e4m3")
    out_0 = np.maximum(h - (h[np.arange(N)[:, None], runs(n3, N)]), 0.5 * (h[np.arange(N)[:, None], runs(n4, N)]))
    return (out_0,) + planes(out_0)

@@ -1,0 +1,218 @@
+from contextlib import ExitStack
+
+import concourse.mybir as mybir
+
+K, T, S, N, H = 512, 2048, 512, 512, 512
+FLOPS = 2 * K * H * S + 2 * H * N * S
+
+F32 = mybir.dt.float32
+BF16 = mybir.dt.bfloat16
+I32 = mybir.dt.int32
+U32 = mybir.dt.uint32
+U16 = mybir.dt.uint16
+U8 = mybir.dt.uint8
+FP8X4 = mybir.dt.float8_e4m3fn_x4
+FP4X4 = mybir.dt.float4_e2m1fn_x4
+ALU = mybir.AluOpType
+ACT = mybir.ActivationFunctionType
+
+P = 128
+PACK = 4
+HALF = S // 2
+HALVES = (slice(0, HALF), slice(HALF, S))
+OUT_CHUNKS = (slice(0, 256), slice(256, 384), slice(384, 512))
+
+
+def entries(lists, cols):
+    return lists[:, cols.start // 16 : cols.stop // 16]
+
+
+def load_scale_rows(queues, tile, scales):
+    for q, queue in enumerate(queues):
+        queue.dma_start(out=tile[32 * q : 32 * q + 4, :].bitcast(I32), in_=scales[0, 4 * q : 4 * q + 4, :].bitcast(I32))
+
+
+def deal_weights(nc, words, scales, raw_words, raw_scales):
+    nc.vector.tensor_copy(
+        out=words[:].rearrange("p (t m b) -> p t m b", t=PACK, b=2),
+        in_=raw_words[:].rearrange("p (m t b) -> p t m b", t=PACK, b=2),
+    )
+    nc.vector.tensor_copy(
+        out=scales[:].rearrange("p (t m) -> p t m", t=PACK),
+        in_=raw_scales[:].rearrange("p (m t) -> p t m", t=PACK),
+    )
+
+
+def product(nc, acc, words, scales, t, codes, code_scales):
+    nc.tensor.matmul_mx(
+        out=acc,
+        lhsT=words[:, 2 * P * t : 2 * P * (t + 1)].bitcast(FP4X4),
+        lhsT_scale=scales[:, P * t : P * (t + 1)],
+        rhs=codes.bitcast(FP8X4),
+        rhs_scale=code_scales,
+        start=True,
+        stop=True,
+    )
+
+
+def round_and_group(copy, grouped, planes):
+    copy(
+        out=grouped[:].rearrange("p (c i t) -> p c t i", i=4, t=PACK),
+        in_=planes[:].rearrange("p t (c i) -> p c t i", i=4),
+    )
+
+
+def tile_picked_sharelay_none_po_kernel(
+    tc, x_words, x_scales, w1_words, w1_scales, gn, w2_words, w2_scales, offs, n1, n2, n3, n4, out_0, out_1, out_2
+):
+    nc = tc.nc
+    with ExitStack() as ctx:
+        keep = ctx.enter_context(tc.tile_pool(name="keep", bufs=1))
+        psum = ctx.enter_context(tc.psum_pool(name="psum", bufs=1))
+
+        def bank(t, c, width):
+            return psum.tile([P, width], F32, name=f"bank{t}{c}", tag=f"bank{t}{c}")
+
+        xw = keep.tile([P, T], U32, align_bytes=64)
+        xs = keep.tile([P, T], U8, align_bytes=64)
+        raw_words = keep.tile([P, 2 * H], U8, align_bytes=64)
+        raw_scales = keep.tile([P, H], U8, align_bytes=64)
+        lists = {}
+        for key in ("offs", "n2", "n1", "n4", "n3"):
+            lists[key] = keep.tile([P, S // 16], U16, name=f"list_{key}")
+        gain = keep.tile([P, PACK], F32)
+        warm = keep.tile([P, 8], F32)
+        warm_out = keep.tile([P, 8], F32)
+
+        nc.gpsimd.memset(xs[:].bitcast(I32), 0)
+        nc.gpsimd.memset(raw_scales[:].bitcast(I32), 0)
+        nc.vector.memset(warm[:], 0.0)
+
+        nc.sync.dma_start(lists["offs"][:], offs)
+        nc.scalar.dma_start(out=xw[:].bitcast(I32), in_=x_words[0].rearrange("p n t -> p (n t)").bitcast(I32))
+        nc.sync.dma_start(out=raw_words[:].bitcast(I32), in_=w1_words[0].bitcast(I32))
+        load_scale_rows([nc.sync] * 4, xs, x_scales)
+        load_scale_rows([nc.sync, nc.sync, nc.gpsimd, nc.gpsimd], raw_scales, w1_scales)
+        nc.sync.dma_start(lists["n2"][:], n2)
+        nc.sync.dma_start(out=gain[:], in_=gn.rearrange("(p t) o -> p (t o)", t=PACK))
+        nc.sync.dma_start(lists["n1"][:], n1)
+        nc.scalar.activation(out=warm_out[:], in_=warm[:], func=ACT.Sigmoid)
+
+        xg_scales = keep.tile([P, S], U8, align_bytes=64)
+        xg_words = keep.tile([P, S], U32, align_bytes=64)
+        w1w = keep.tile([P, 2 * H], U8, align_bytes=64)
+        w1s = keep.tile([P, H], U8, align_bytes=64)
+        nc.vector.tensor_copy(out=xg_scales[:], in_=xs[:].indirect(lists["offs"][:]))
+        deal_weights(nc, w1w, w1s, raw_words, raw_scales)
+        for cols in HALVES:
+            nc.vector.tensor_copy(out=xg_words[:, cols], in_=xw[:].indirect(entries(lists["offs"], cols)))
+
+        nc.sync.dma_start(out=raw_words[:].bitcast(I32), in_=w2_words[0].bitcast(I32))
+        load_scale_rows([nc.sync] * 4, raw_scales, w2_scales)
+        nc.sync.dma_start(lists["n4"][:], n4)
+        nc.sync.dma_start(lists["n3"][:], n3)
+
+        y_win = [keep.tile([P, S], F32, name=f"y_win{t}") for t in range(PACK)]
+        y_own = [keep.tile([P, S], F32, name=f"y_own{t}") for t in range(PACK)]
+        gy_win = [keep.tile([P, S], F32, name=f"gy_win{t}") for t in range(PACK)]
+        diff = [keep.tile([P, S], F32, name=f"diff{t}") for t in range(PACK)]
+        share = [keep.tile([P, S], F32, name=f"share{t}") for t in range(PACK)]
+        pieces = []
+        for t in range(PACK):
+            pieces.append([])
+            for c, cols in enumerate(HALVES if t == 0 else (slice(0, S),)):
+                acc = bank(t, c, cols.stop - cols.start)
+                product(nc, acc[:], w1w, w1s, t, xg_words[:, cols], xg_scales[:, cols])
+                pieces[t].append((cols, acc))
+
+        nc.scalar.copy(out=y_win[0][:, HALVES[0]], in_=pieces[0][0][1][:])
+        nc.vector.tensor_copy(out=y_win[0][:, HALVES[1]], in_=pieces[0][1][1][:])
+        for t in range(PACK):
+            for cols, acc in pieces[t]:
+                if t > 0:
+                    nc.scalar.copy(out=y_win[t][:, cols], in_=acc[:])
+                nc.scalar.copy(out=y_own[t][:, cols], in_=acc[:])
+            for cols in HALVES:
+                nc.vector.tensor_tensor(
+                    out=diff[t][:, cols],
+                    in0=y_win[t][:].indirect(entries(lists["n2"], cols)),
+                    in1=y_own[t][:, cols],
+                    op=ALU.subtract,
+                )
+
+        w2w = keep.tile([P, 2 * N], U8, align_bytes=64)
+        w2s = keep.tile([P, N], U8, align_bytes=64)
+        deal_weights(nc, w2w, w2s, raw_words, raw_scales)
+
+        z = [keep.tile([P, PACK, HALF], F32, name=f"z{c}") for c in range(2)]
+        for c, cols in enumerate(HALVES):
+            for t in range(PACK):
+                nc.scalar.activation(out=share[t][:, cols], in_=diff[t][:, cols], func=ACT.Sigmoid, scale=-0.5)
+                if c == 0:
+                    for part, acc in pieces[t]:
+                        nc.scalar.activation(out=gy_win[t][:, part], in_=acc[:], func=ACT.Copy, scale=gain[:, t : t + 1])
+                nc.vector.tensor_tensor(
+                    out=z[c][:, t, :],
+                    in0=gy_win[t][:].indirect(entries(lists["n1"], cols)),
+                    in1=share[t][:, cols],
+                    op=ALU.mult,
+                )
+
+        z_words = [keep.tile([P, HALF], U32, name=f"z_words{c}", align_bytes=64) for c in range(2)]
+        z_scales = [keep.tile([P, HALF], U8, name=f"z_scales{c}", align_bytes=64) for c in range(2)]
+        z_bf = [keep.tile([P, PACK * HALF], BF16, name=f"z_bf{c}", align_bytes=64) for c in range(2)]
+        round_and_group(nc.scalar.copy, z_bf[0], z[0])
+        round_and_group(nc.vector.tensor_copy, z_bf[1], z[1])
+        for c in range(2):
+            nc.vector.quantize_mx(out=z_words[c][:].bitcast(FP8X4), scales=z_scales[c][:], in_=z_bf[c][:])
+
+        nh_win = [keep.tile([P, S], F32, name=f"nh_win{t}") for t in range(PACK)]
+        h_own = [keep.tile([P, S], F32, name=f"h_own{t}") for t in range(PACK)]
+        h_acc = [[None, None] for t in range(PACK)]
+        for t in range(PACK):
+            for c in range(2):
+                h_acc[t][c] = bank(t, c, HALF)
+                product(nc, h_acc[t][c][:], w2w, w2s, t, z_words[c][:], z_scales[c][:])
+        for t in range(PACK):
+            for c, cols in enumerate(HALVES):
+                if t == 0 and c == 1:
+                    nc.vector.tensor_scalar(
+                        out=nh_win[t][:, cols], in0=h_acc[t][c][:], scalar1=-1.0, scalar2=None, op0=ALU.mult
+                    )
+                else:
+                    nc.scalar.activation(out=nh_win[t][:, cols], in_=h_acc[t][c][:], func=ACT.Copy, scale=-1.0)
+            nc.scalar.copy(out=h_own[t][:, HALVES[0]], in_=h_acc[t][0][:])
+        for t in range(PACK):
+            nc.scalar.copy(out=h_own[t][:, HALVES[1]], in_=h_acc[t][1][:])
+
+        out_rows = out_0.rearrange("(p t) s -> p t s", t=PACK)
+        out_words = out_1[0].rearrange("p n t -> p (n t)").bitcast(I32)
+        res_scales = keep.tile([P, S], U8, align_bytes=64)
+        last = len(OUT_CHUNKS) - 1
+        for c, cols in enumerate(OUT_CHUNKS):
+            width = cols.stop - cols.start
+            far = keep.tile([P, PACK, width], F32, name=f"far{c}")
+            gap = keep.tile([P, PACK, width], F32, name=f"gap{c}")
+            res = keep.tile([P, PACK, width], F32, name=f"res{c}")
+            for t in range(PACK):
+                nc.vector.tensor_copy(out=far[:, t, :], in_=nh_win[t][:].indirect(entries(lists["n4"], cols)))
+                nc.vector.tensor_tensor(
+                    out=gap[:, t, :],
+                    in0=nh_win[t][:].indirect(entries(lists["n3"], cols)),
+                    in1=h_own[t][:, cols],
+                    op=ALU.add,
+                )
+            nc.vector.scalar_tensor_tensor(
+                out=res[:], in0=far[:], scalar=-0.5, in1=gap[:], op0=ALU.mult, op1=ALU.max
+            )
+            nc.sync.dma_start(out=out_rows[:, :, cols], in_=res[:])
+            res_bf = keep.tile([P, PACK * width], BF16, name=f"res_bf{c}", align_bytes=64)
+            res_words = keep.tile([P, width], U32, name=f"res_words{c}", align_bytes=64)
+            round_and_group(nc.vector.tensor_copy if c == last else nc.scalar.copy, res_bf, res)
+            nc.vector.quantize_mx(out=res_words[:].bitcast(FP8X4), scales=res_scales[:, cols], in_=res_bf[:])
+            nc.sync.dma_start(out=out_words[:, cols], in_=res_words[:].bitcast(I32))
+        for q in range(4):
+            queue = nc.scalar if q % 2 else nc.sync
+            queue.dma_start(
+                out=out_2[0, 4 * q : 4 * q + 4, :].bitcast(I32), in_=res_scales[32 * q : 32 * q + 4, :].bitcast(I32)
+            )

@@ -20,7 +20,8 @@ P = 128
 PACK = 4
 HALF = S // 2
 HALVES = (slice(0, HALF), slice(HALF, S))
-OUT_CHUNKS = (slice(0, 256), slice(256, 384), slice(384, 512))
+WHOLE = slice(0, S)
+SPARE = slice(S, 2 * S)
 
 
 def entries(lists, cols):
@@ -32,11 +33,14 @@ def load_scale_rows(queues, tile, scales):
         queue.dma_start(out=tile[32 * q : 32 * q + 4, :].bitcast(I32), in_=scales[0, 4 * q : 4 * q + 4, :].bitcast(I32))
 
 
-def deal_weights(nc, words, scales, raw_words, raw_scales):
+def deal_words(nc, words, raw_words):
     nc.vector.tensor_copy(
         out=words[:].rearrange("p (t m b) -> p t m b", t=PACK, b=2),
         in_=raw_words[:].rearrange("p (m t b) -> p t m b", t=PACK, b=2),
     )
+
+
+def deal_scales(nc, scales, raw_scales):
     nc.vector.tensor_copy(
         out=scales[:].rearrange("p (t m) -> p t m", t=PACK),
         in_=raw_scales[:].rearrange("p (m t) -> p t m", t=PACK),
@@ -58,7 +62,7 @@ def product(nc, acc, words, scales, t, codes, code_scales):
 def round_and_group(copy, grouped, planes):
     copy(
         out=grouped[:].rearrange("p (c i t) -> p c t i", i=4, t=PACK),
-        in_=planes[:].rearrange("p t (c i) -> p c t i", i=4),
+        in_=planes.rearrange("p t (c i) -> p c t i", i=4),
     )
 
 
@@ -70,13 +74,12 @@ def tile_picked_sharelay_none_po_kernel(
         keep = ctx.enter_context(tc.tile_pool(name="keep", bufs=1))
         psum = ctx.enter_context(tc.psum_pool(name="psum", bufs=1))
 
-        def bank(t, c, width):
-            return psum.tile([P, width], F32, name=f"bank{t}{c}", tag=f"bank{t}{c}")
-
         xw = keep.tile([P, T], U32, align_bytes=64)
         xs = keep.tile([P, T], U8, align_bytes=64)
         raw_words = keep.tile([P, 2 * H], U8, align_bytes=64)
-        raw_scales = keep.tile([P, H], U8, align_bytes=64)
+        raw_words2 = keep.tile([P, 2 * N], U8, align_bytes=64)
+        raw_scales = keep.tile([P, H], U8, align_bytes=64, tag="w1_scales_then_w2_words")
+        raw_scales2 = keep.tile([P, N], U8, align_bytes=64)
         lists = {}
         for key in ("offs", "n2", "n1", "n4", "n3"):
             lists[key] = keep.tile([P, S // 16], U16, name=f"list_{key}")
@@ -84,15 +87,17 @@ def tile_picked_sharelay_none_po_kernel(
         warm = keep.tile([P, 8], F32)
         warm_out = keep.tile([P, 8], F32)
 
-        nc.gpsimd.memset(xs[:].bitcast(I32), 0)
+        nc.vector.memset(xs[:].bitcast(I32), 0)
         nc.gpsimd.memset(raw_scales[:].bitcast(I32), 0)
         nc.vector.memset(warm[:], 0.0)
+        nc.vector.memset(raw_scales2[:].bitcast(I32), 0)
 
         nc.sync.dma_start(lists["offs"][:], offs)
-        nc.scalar.dma_start(out=xw[:].bitcast(I32), in_=x_words[0].rearrange("p n t -> p (n t)").bitcast(I32))
         nc.sync.dma_start(out=raw_words[:].bitcast(I32), in_=w1_words[0].bitcast(I32))
-        load_scale_rows([nc.sync] * 4, xs, x_scales)
-        load_scale_rows([nc.sync, nc.sync, nc.gpsimd, nc.gpsimd], raw_scales, w1_scales)
+        nc.sync.dma_start(out=xw[:].bitcast(I32), in_=x_words[0].rearrange("p n t -> p (n t)").bitcast(I32))
+        load_scale_rows([nc.scalar] * 4, xs, x_scales)
+        load_scale_rows([nc.gpsimd, nc.gpsimd, nc.gpsimd, nc.scalar], raw_scales, w1_scales)
+        nc.sync.dma_start(out=raw_words2[:].bitcast(I32), in_=w2_words[0].bitcast(I32))
         nc.sync.dma_start(lists["n2"][:], n2)
         nc.sync.dma_start(out=gain[:], in_=gn.rearrange("(p t) o -> p (t o)", t=PACK))
         nc.sync.dma_start(lists["n1"][:], n1)
@@ -103,36 +108,44 @@ def tile_picked_sharelay_none_po_kernel(
         w1w = keep.tile([P, 2 * H], U8, align_bytes=64)
         w1s = keep.tile([P, H], U8, align_bytes=64)
         nc.vector.tensor_copy(out=xg_scales[:], in_=xs[:].indirect(lists["offs"][:]))
-        deal_weights(nc, w1w, w1s, raw_words, raw_scales)
+        deal_words(nc, w1w, raw_words)
+        deal_scales(nc, w1s, raw_scales)
         for cols in HALVES:
             nc.vector.tensor_copy(out=xg_words[:, cols], in_=xw[:].indirect(entries(lists["offs"], cols)))
+        w2w = keep.tile([P, 2 * N], U8, align_bytes=64, tag="w1_scales_then_w2_words")
+        deal_words(nc, w2w, raw_words2)
 
-        nc.sync.dma_start(out=raw_words[:].bitcast(I32), in_=w2_words[0].bitcast(I32))
-        load_scale_rows([nc.sync] * 4, raw_scales, w2_scales)
+        load_scale_rows([nc.sync] * 4, raw_scales2, w2_scales)
         nc.sync.dma_start(lists["n4"][:], n4)
         nc.sync.dma_start(lists["n3"][:], n3)
 
-        y_win = [keep.tile([P, S], F32, name=f"y_win{t}") for t in range(PACK)]
-        y_own = [keep.tile([P, S], F32, name=f"y_own{t}") for t in range(PACK)]
-        gy_win = [keep.tile([P, S], F32, name=f"gy_win{t}") for t in range(PACK)]
-        diff = [keep.tile([P, S], F32, name=f"diff{t}") for t in range(PACK)]
+        y_win = [keep.tile([P, S if t == 0 else 2 * S], F32, name=f"y_win{t}") for t in range(PACK)]
+        y_last = keep.tile([P, S], F32)
+        y_own = [y_win[t + 1][:, SPARE] for t in range(PACK - 1)] + [y_last[:]]
+        win = [keep.tile([P, 2 * S], F32, name=f"win{t}") for t in range(PACK)]
+        diff = [win[t][:, SPARE] for t in range(PACK)]
         share = [keep.tile([P, S], F32, name=f"share{t}") for t in range(PACK)]
-        pieces = []
-        for t in range(PACK):
-            pieces.append([])
-            for c, cols in enumerate(HALVES if t == 0 else (slice(0, S),)):
-                acc = bank(t, c, cols.stop - cols.start)
-                product(nc, acc[:], w1w, w1s, t, xg_words[:, cols], xg_scales[:, cols])
-                pieces[t].append((cols, acc))
 
-        nc.scalar.copy(out=y_win[0][:, HALVES[0]], in_=pieces[0][0][1][:])
-        nc.vector.tensor_copy(out=y_win[0][:, HALVES[1]], in_=pieces[0][1][1][:])
-        for t in range(PACK):
-            for cols, acc in pieces[t]:
+        def products(words, scales, codes, code_scales):
+            pieces = []
+            for t in range(PACK):
+                pieces.append([])
+                for c, cols in enumerate(HALVES if t == 0 else (WHOLE,)):
+                    acc = psum.tile([P, cols.stop - cols.start], F32, name=f"bank{t}{c}", tag=f"bank{t}{c}", bufs=2 if t > 0 else 1)
+                    product(nc, acc[:], words, scales, t, codes[:, cols], code_scales[:, cols])
+                    pieces[t].append((cols, acc))
+            return pieces
+
+        y_acc = products(w1w, w1s, xg_words, xg_scales)
+
+        w2s = keep.tile([P, N], U8, align_bytes=64)
+        z_all = keep.tile([P, PACK, S], F32)
+
+        def differences(t):
+            for cols, acc in y_acc[t]:
                 if t > 0:
                     nc.scalar.copy(out=y_win[t][:, cols], in_=acc[:])
                 nc.scalar.copy(out=y_own[t][:, cols], in_=acc[:])
-            for cols in HALVES:
                 nc.vector.tensor_tensor(
                     out=diff[t][:, cols],
                     in0=y_win[t][:].indirect(entries(lists["n2"], cols)),
@@ -140,77 +153,82 @@ def tile_picked_sharelay_none_po_kernel(
                     op=ALU.subtract,
                 )
 
-        w2w = keep.tile([P, 2 * N], U8, align_bytes=64)
-        w2s = keep.tile([P, N], U8, align_bytes=64)
-        deal_weights(nc, w2w, w2s, raw_words, raw_scales)
-
-        z = [keep.tile([P, PACK, HALF], F32, name=f"z{c}") for c in range(2)]
-        for c, cols in enumerate(HALVES):
-            for t in range(PACK):
+        def shares(t):
+            parts = HALVES if t == PACK - 1 else (WHOLE,)
+            for part, acc in y_acc[t]:
+                nc.scalar.activation(out=win[t][:, part], in_=acc[:], func=ACT.Copy, scale=gain[:, t : t + 1])
+            for cols in parts:
                 nc.scalar.activation(out=share[t][:, cols], in_=diff[t][:, cols], func=ACT.Sigmoid, scale=-0.5)
-                if c == 0:
-                    for part, acc in pieces[t]:
-                        nc.scalar.activation(out=gy_win[t][:, part], in_=acc[:], func=ACT.Copy, scale=gain[:, t : t + 1])
+            for cols in parts:
                 nc.vector.tensor_tensor(
-                    out=z[c][:, t, :],
-                    in0=gy_win[t][:].indirect(entries(lists["n1"], cols)),
+                    out=z_all[:, t, cols],
+                    in0=win[t][:].indirect(entries(lists["n1"], cols)),
                     in1=share[t][:, cols],
                     op=ALU.mult,
                 )
 
-        z_words = [keep.tile([P, HALF], U32, name=f"z_words{c}", align_bytes=64) for c in range(2)]
-        z_scales = [keep.tile([P, HALF], U8, name=f"z_scales{c}", align_bytes=64) for c in range(2)]
-        z_bf = [keep.tile([P, PACK * HALF], BF16, name=f"z_bf{c}", align_bytes=64) for c in range(2)]
-        round_and_group(nc.scalar.copy, z_bf[0], z[0])
-        round_and_group(nc.vector.tensor_copy, z_bf[1], z[1])
-        for c in range(2):
-            nc.vector.quantize_mx(out=z_words[c][:].bitcast(FP8X4), scales=z_scales[c][:], in_=z_bf[c][:])
+        nc.scalar.copy(out=y_win[0][:, HALVES[0]], in_=y_acc[0][0][1][:])
+        nc.vector.tensor_copy(out=y_win[0][:, HALVES[1]], in_=y_acc[0][1][1][:])
+        differences(0)
+        differences(1)
+        differences(2)
+        shares(0)
+        differences(3)
+        deal_scales(nc, w2s, raw_scales2)
+        shares(1)
+        shares(2)
+        shares(3)
 
-        nh_win = [keep.tile([P, S], F32, name=f"nh_win{t}") for t in range(PACK)]
-        h_own = [keep.tile([P, S], F32, name=f"h_own{t}") for t in range(PACK)]
-        h_acc = [[None, None] for t in range(PACK)]
-        for t in range(PACK):
-            for c in range(2):
-                h_acc[t][c] = bank(t, c, HALF)
-                product(nc, h_acc[t][c][:], w2w, w2s, t, z_words[c][:], z_scales[c][:])
-        for t in range(PACK):
+        def quantise(planes, tag):
+            words = keep.tile([P, S], U32, name=f"{tag}_words", align_bytes=64)
+            scales = keep.tile([P, S], U8, name=f"{tag}_scales", align_bytes=64)
+            grouped = [keep.tile([P, PACK * HALF], BF16, name=f"{tag}_bf{c}", align_bytes=64) for c in range(2)]
+            round_and_group(nc.scalar.copy, grouped[0], planes[:, :, HALVES[0]])
+            round_and_group(nc.vector.tensor_copy, grouped[1], planes[:, :, HALVES[1]])
             for c, cols in enumerate(HALVES):
-                if t == 0 and c == 1:
-                    nc.vector.tensor_scalar(
-                        out=nh_win[t][:, cols], in0=h_acc[t][c][:], scalar1=-1.0, scalar2=None, op0=ALU.mult
-                    )
-                else:
-                    nc.scalar.activation(out=nh_win[t][:, cols], in_=h_acc[t][c][:], func=ACT.Copy, scale=-1.0)
-            nc.scalar.copy(out=h_own[t][:, HALVES[0]], in_=h_acc[t][0][:])
-        for t in range(PACK):
-            nc.scalar.copy(out=h_own[t][:, HALVES[1]], in_=h_acc[t][1][:])
+                nc.vector.quantize_mx(out=words[:, cols].bitcast(FP8X4), scales=scales[:, cols], in_=grouped[c][:])
+            return words, scales
 
+        z_words, z_scales = quantise(z_all, "z")
+        h_acc = products(w2w, w2s, z_words, z_scales)
+
+        h_own = [keep.tile([P, S], F32, name=f"h_own{t}") for t in range(PACK)]
+        far = keep.tile([P, PACK, S], F32)
+        gap = keep.tile([P, PACK, S], F32)
+        res = keep.tile([P, PACK, S], F32)
         out_rows = out_0.rearrange("(p t) s -> p t s", t=PACK)
-        out_words = out_1[0].rearrange("p n t -> p (n t)").bitcast(I32)
-        res_scales = keep.tile([P, S], U8, align_bytes=64)
-        last = len(OUT_CHUNKS) - 1
-        for c, cols in enumerate(OUT_CHUNKS):
-            width = cols.stop - cols.start
-            far = keep.tile([P, PACK, width], F32, name=f"far{c}")
-            gap = keep.tile([P, PACK, width], F32, name=f"gap{c}")
-            res = keep.tile([P, PACK, width], F32, name=f"res{c}")
-            for t in range(PACK):
-                nc.vector.tensor_copy(out=far[:, t, :], in_=nh_win[t][:].indirect(entries(lists["n4"], cols)))
-                nc.vector.tensor_tensor(
-                    out=gap[:, t, :],
-                    in0=nh_win[t][:].indirect(entries(lists["n3"], cols)),
-                    in1=h_own[t][:, cols],
-                    op=ALU.add,
-                )
+        nc.vector.tensor_scalar(
+            out=win[0][:, HALVES[1]], in0=h_acc[0][1][1][:], scalar1=-1.0, scalar2=None, op0=ALU.mult
+        )
+        for t in range(PACK):
+            for cols, acc in h_acc[t][:1]:
+                nc.scalar.activation(out=win[t][:, cols], in_=acc[:], func=ACT.Copy, scale=-1.0)
+            for cols, acc in h_acc[t]:
+                nc.scalar.copy(out=h_own[t][:, cols], in_=acc[:])
+
+        def larger(t, cols):
             nc.vector.scalar_tensor_tensor(
-                out=res[:], in0=far[:], scalar=-0.5, in1=gap[:], op0=ALU.mult, op1=ALU.max
+                out=res[:, t, cols], in0=far[:, t, cols], scalar=-0.5, in1=gap[:, t, cols], op0=ALU.mult, op1=ALU.max
             )
-            nc.sync.dma_start(out=out_rows[:, :, cols], in_=res[:])
-            res_bf = keep.tile([P, PACK * width], BF16, name=f"res_bf{c}", align_bytes=64)
-            res_words = keep.tile([P, width], U32, name=f"res_words{c}", align_bytes=64)
-            round_and_group(nc.vector.tensor_copy if c == last else nc.scalar.copy, res_bf, res)
-            nc.vector.quantize_mx(out=res_words[:].bitcast(FP8X4), scales=res_scales[:, cols], in_=res_bf[:])
-            nc.sync.dma_start(out=out_words[:, cols], in_=res_words[:].bitcast(I32))
+            nc.sync.dma_start(out=out_rows[:, t, cols], in_=res[:, t, cols])
+
+        steps = [(t, WHOLE) for t in range(PACK - 1)] + [(PACK - 1, cols) for cols in HALVES]
+        for i, (t, cols) in enumerate(steps):
+            nc.vector.tensor_copy(out=far[:, t, cols], in_=win[t][:].indirect(entries(lists["n4"], cols)))
+            if i > 0:
+                larger(*steps[i - 1])
+            nc.vector.tensor_tensor(
+                out=gap[:, t, cols],
+                in0=win[t][:].indirect(entries(lists["n3"], cols)),
+                in1=h_own[t][:, cols],
+                op=ALU.add,
+            )
+        larger(*steps[-1])
+
+        res_words, res_scales = quantise(res, "res")
+        out_words = out_1[0].rearrange("p n t -> p (n t)").bitcast(I32)
+        for cols in HALVES:
+            nc.sync.dma_start(out=out_words[:, cols], in_=res_words[:, cols].bitcast(I32))
         for q in range(4):
             queue = nc.scalar if q % 2 else nc.sync
             queue.dma_start(

@@ -95,10 +95,10 @@ def tile_picked_sharelay_none_po_kernel(
         nc.sync.dma_start(lists["offs"][:], offs)
         nc.sync.dma_start(out=raw_words[:].bitcast(I32), in_=w1_words[0].bitcast(I32))
         nc.sync.dma_start(out=xw[:].bitcast(I32), in_=x_words[0].rearrange("p n t -> p (n t)").bitcast(I32))
+        load_scale_rows([nc.scalar, nc.sync, nc.sync, nc.sync], raw_scales, w1_scales)
         load_scale_rows([nc.scalar] * 4, xs, x_scales)
-        load_scale_rows([nc.gpsimd, nc.gpsimd, nc.gpsimd, nc.scalar], raw_scales, w1_scales)
-        nc.sync.dma_start(out=raw_words2[:].bitcast(I32), in_=w2_words[0].bitcast(I32))
         nc.sync.dma_start(lists["n2"][:], n2)
+        nc.sync.dma_start(out=raw_words2[:].bitcast(I32), in_=w2_words[0].bitcast(I32))
         nc.sync.dma_start(out=gain[:], in_=gn.rearrange("(p t) o -> p (t o)", t=PACK))
         nc.sync.dma_start(lists["n1"][:], n1)
         nc.scalar.activation(out=warm_out[:], in_=warm[:], func=ACT.Sigmoid)

from contextlib import ExitStack

import concourse.mybir as mybir

K, T, S, N, H = 512, 2048, 512, 512, 512
FLOPS = 2 * K * H * S + 2 * H * N * S

F32 = mybir.dt.float32
BF16 = mybir.dt.bfloat16
I32 = mybir.dt.int32
U32 = mybir.dt.uint32
U16 = mybir.dt.uint16
U8 = mybir.dt.uint8
FP8X4 = mybir.dt.float8_e4m3fn_x4
FP4X4 = mybir.dt.float4_e2m1fn_x4
ALU = mybir.AluOpType
ACT = mybir.ActivationFunctionType

P = 128
PACK = 4
HALF = S // 2
HALVES = (slice(0, HALF), slice(HALF, S))
WHOLE = slice(0, S)
SPARE = slice(S, 2 * S)


def entries(lists, cols):
    return lists[:, cols.start // 16 : cols.stop // 16]


def load_scale_rows(queues, tile, scales):
    for q, queue in enumerate(queues):
        queue.dma_start(out=tile[32 * q : 32 * q + 4, :].bitcast(I32), in_=scales[0, 4 * q : 4 * q + 4, :].bitcast(I32))


def deal_words(nc, words, raw_words):
    nc.vector.tensor_copy(
        out=words[:].rearrange("p (t m b) -> p t m b", t=PACK, b=2),
        in_=raw_words[:].rearrange("p (m t b) -> p t m b", t=PACK, b=2),
    )


def deal_scales(nc, scales, raw_scales):
    nc.vector.tensor_copy(
        out=scales[:].rearrange("p (t m) -> p t m", t=PACK),
        in_=raw_scales[:].rearrange("p (m t) -> p t m", t=PACK),
    )


def product(nc, acc, words, scales, t, codes, code_scales):
    nc.tensor.matmul_mx(
        out=acc,
        lhsT=words[:, 2 * P * t : 2 * P * (t + 1)].bitcast(FP4X4),
        lhsT_scale=scales[:, P * t : P * (t + 1)],
        rhs=codes.bitcast(FP8X4),
        rhs_scale=code_scales,
        start=True,
        stop=True,
    )


def round_and_group(copy, grouped, planes):
    copy(
        out=grouped[:].rearrange("p (c i t) -> p c t i", i=4, t=PACK),
        in_=planes.rearrange("p t (c i) -> p c t i", i=4),
    )


def tile_picked_sharelay_none_po_kernel(
    tc, x_words, x_scales, w1_words, w1_scales, gn, w2_words, w2_scales, offs, n1, n2, n3, n4, out_0, out_1, out_2
):
    nc = tc.nc
    with ExitStack() as ctx:
        keep = ctx.enter_context(tc.tile_pool(name="keep", bufs=1))
        psum = ctx.enter_context(tc.psum_pool(name="psum", bufs=1))

        xw = keep.tile([P, T], U32, align_bytes=64)
        xs = keep.tile([P, T], U8, align_bytes=64)
        raw_words = keep.tile([P, 2 * H], U8, align_bytes=64)
        raw_words2 = keep.tile([P, 2 * N], U8, align_bytes=64)
        raw_scales = keep.tile([P, H], U8, align_bytes=64, tag="w1_scales_then_w2_words")
        raw_scales2 = keep.tile([P, N], U8, align_bytes=64)
        lists = {}
        for key in ("offs", "n2", "n1", "n4", "n3"):
            lists[key] = keep.tile([P, S // 16], U16, name=f"list_{key}")
        gain = keep.tile([P, PACK], F32)
        warm = keep.tile([P, 8], F32)
        warm_out = keep.tile([P, 8], F32)

        nc.vector.memset(xs[:].bitcast(I32), 0)
        nc.gpsimd.memset(raw_scales[:].bitcast(I32), 0)
        nc.vector.memset(warm[:], 0.0)
        nc.vector.memset(raw_scales2[:].bitcast(I32), 0)

        nc.sync.dma_start(lists["offs"][:], offs)
        nc.sync.dma_start(out=raw_words[:].bitcast(I32), in_=w1_words[0].bitcast(I32))
        nc.sync.dma_start(out=xw[:].bitcast(I32), in_=x_words[0].rearrange("p n t -> p (n t)").bitcast(I32))
        load_scale_rows([nc.scalar, nc.sync, nc.sync, nc.sync], raw_scales, w1_scales)
        load_scale_rows([nc.scalar] * 4, xs, x_scales)
        nc.sync.dma_start(lists["n2"][:], n2)
        nc.sync.dma_start(out=raw_words2[:].bitcast(I32), in_=w2_words[0].bitcast(I32))
        nc.sync.dma_start(out=gain[:], in_=gn.rearrange("(p t) o -> p (t o)", t=PACK))
        nc.sync.dma_start(lists["n1"][:], n1)
        nc.scalar.activation(out=warm_out[:], in_=warm[:], func=ACT.Sigmoid)

        xg_scales = keep.tile([P, S], U8, align_bytes=64)
        xg_words = keep.tile([P, S], U32, align_bytes=64)
        w1w = keep.tile([P, 2 * H], U8, align_bytes=64)
        w1s = keep.tile([P, H], U8, align_bytes=64)
        nc.vector.tensor_copy(out=xg_scales[:], in_=xs[:].indirect(lists["offs"][:]))
        deal_words(nc, w1w, raw_words)
        deal_scales(nc, w1s, raw_scales)
        for cols in HALVES:
            nc.vector.tensor_copy(out=xg_words[:, cols], in_=xw[:].indirect(entries(lists["offs"], cols)))
        w2w = keep.tile([P, 2 * N], U8, align_bytes=64, tag="w1_scales_then_w2_words")
        deal_words(nc, w2w, raw_words2)

        load_scale_rows([nc.sync] * 4, raw_scales2, w2_scales)
        nc.sync.dma_start(lists["n4"][:], n4)
        nc.sync.dma_start(lists["n3"][:], n3)

        y_win = [keep.tile([P, S if t == 0 else 2 * S], F32, name=f"y_win{t}") for t in range(PACK)]
        y_last = keep.tile([P, S], F32)
        y_own = [y_win[t + 1][:, SPARE] for t in range(PACK - 1)] + [y_last[:]]
        win = [keep.tile([P, 2 * S], F32, name=f"win{t}") for t in range(PACK)]
        diff = [win[t][:, SPARE] for t in range(PACK)]
        share = [keep.tile([P, S], F32, name=f"share{t}") for t in range(PACK)]

        def products(words, scales, codes, code_scales):
            pieces = []
            for t in range(PACK):
                pieces.append([])
                for c, cols in enumerate(HALVES if t == 0 else (WHOLE,)):
                    acc = psum.tile([P, cols.stop - cols.start], F32, name=f"bank{t}{c}", tag=f"bank{t}{c}", bufs=2 if t > 0 else 1)
                    product(nc, acc[:], words, scales, t, codes[:, cols], code_scales[:, cols])
                    pieces[t].append((cols, acc))
            return pieces

        y_acc = products(w1w, w1s, xg_words, xg_scales)

        w2s = keep.tile([P, N], U8, align_bytes=64)
        z_all = keep.tile([P, PACK, S], F32)

        def differences(t):
            for cols, acc in y_acc[t]:
                if t > 0:
                    nc.scalar.copy(out=y_win[t][:, cols], in_=acc[:])
                nc.scalar.copy(out=y_own[t][:, cols], in_=acc[:])
                nc.vector.tensor_tensor(
                    out=diff[t][:, cols],
                    in0=y_win[t][:].indirect(entries(lists["n2"], cols)),
                    in1=y_own[t][:, cols],
                    op=ALU.subtract,
                )

        def shares(t):
            parts = HALVES if t == PACK - 1 else (WHOLE,)
            for part, acc in y_acc[t]:
                nc.scalar.activation(out=win[t][:, part], in_=acc[:], func=ACT.Copy, scale=gain[:, t : t + 1])
            for cols in parts:
                nc.scalar.activation(out=share[t][:, cols], in_=diff[t][:, cols], func=ACT.Sigmoid, scale=-0.5)
            for cols in parts:
                nc.vector.tensor_tensor(
                    out=z_all[:, t, cols],
                    in0=win[t][:].indirect(entries(lists["n1"], cols)),
                    in1=share[t][:, cols],
                    op=ALU.mult,
                )

        nc.scalar.copy(out=y_win[0][:, HALVES[0]], in_=y_acc[0][0][1][:])
        nc.vector.tensor_copy(out=y_win[0][:, HALVES[1]], in_=y_acc[0][1][1][:])
        differences(0)
        differences(1)
        differences(2)
        shares(0)
        differences(3)
        deal_scales(nc, w2s, raw_scales2)
        shares(1)
        shares(2)
        shares(3)

        def quantise(planes, tag):
            words = keep.tile([P, S], U32, name=f"{tag}_words", align_bytes=64)
            scales = keep.tile([P, S], U8, name=f"{tag}_scales", align_bytes=64)
            grouped = [keep.tile([P, PACK * HALF], BF16, name=f"{tag}_bf{c}", align_bytes=64) for c in range(2)]
            round_and_group(nc.scalar.copy, grouped[0], planes[:, :, HALVES[0]])
            round_and_group(nc.vector.tensor_copy, grouped[1], planes[:, :, HALVES[1]])
            for c, cols in enumerate(HALVES):
                nc.vector.quantize_mx(out=words[:, cols].bitcast(FP8X4), scales=scales[:, cols], in_=grouped[c][:])
            return words, scales

        z_words, z_scales = quantise(z_all, "z")
        h_acc = products(w2w, w2s, z_words, z_scales)

        h_own = [keep.tile([P, S], F32, name=f"h_own{t}") for t in range(PACK)]
        far = keep.tile([P, PACK, S], F32)
        gap = keep.tile([P, PACK, S], F32)
        res = keep.tile([P, PACK, S], F32)
        out_rows = out_0.rearrange("(p t) s -> p t s", t=PACK)
        nc.vector.tensor_scalar(
            out=win[0][:, HALVES[1]], in0=h_acc[0][1][1][:], scalar1=-1.0, scalar2=None, op0=ALU.mult
        )
        for t in range(PACK):
            for cols, acc in h_acc[t][:1]:
                nc.scalar.activation(out=win[t][:, cols], in_=acc[:], func=ACT.Copy, scale=-1.0)
            for cols, acc in h_acc[t]:
                nc.scalar.copy(out=h_own[t][:, cols], in_=acc[:])

        def larger(t, cols):
            nc.vector.scalar_tensor_tensor(
                out=res[:, t, cols], in0=far[:, t, cols], scalar=-0.5, in1=gap[:, t, cols], op0=ALU.mult, op1=ALU.max
            )
            nc.sync.dma_start(out=out_rows[:, t, cols], in_=res[:, t, cols])

        steps = [(t, WHOLE) for t in range(PACK - 1)] + [(PACK - 1, cols) for cols in HALVES]
        for i, (t, cols) in enumerate(steps):
            nc.vector.tensor_copy(out=far[:, t, cols], in_=win[t][:].indirect(entries(lists["n4"], cols)))
            if i > 0:
                larger(*steps[i - 1])
            nc.vector.tensor_tensor(
                out=gap[:, t, cols],
                in0=win[t][:].indirect(entries(lists["n3"], cols)),
                in1=h_own[t][:, cols],
                op=ALU.add,
            )
        larger(*steps[-1])

        res_words, res_scales = quantise(res, "res")
        out_words = out_1[0].rearrange("p n t -> p (n t)").bitcast(I32)
        for cols in HALVES:
            nc.sync.dma_start(out=out_words[:, cols], in_=res_words[:, cols].bitcast(I32))
        for q in range(4):
            queue = nc.scalar if q % 2 else nc.sync
            queue.dma_start(
                out=out_2[0, 4 * q : 4 * q + 4, :].bitcast(I32), in_=res_scales[32 * q : 32 * q + 4, :].bitcast(I32)
            )
